import numpy as np
import ml_dtypes


def mxq(x, axis, fmt="e4m3"):
    dtype, down = {"e4m3": (ml_dtypes.float8_e4m3fn, 7), "e5m2": (ml_dtypes.float8_e5m2, 14)}[fmt]
    v = np.moveaxis(np.asarray(x, np.float32).astype(ml_dtypes.bfloat16).astype(np.float64), axis, -1)
    blocks = v.reshape(v.shape[:-1] + (-1, 32))
    amax = np.abs(blocks).max(-1, keepdims=True)
    byte = np.maximum(np.where(amax > 0, np.frexp(amax)[1] - 1 + 127, 0) - down, 1)
    scale = np.exp2(byte - 127.0)
    codes = (blocks / scale).astype(np.float32).astype(dtype).astype(np.float64)
    return np.moveaxis((codes * scale).reshape(v.shape), -1, axis)


WIDE = False


def mx_kscale(k):
    if not WIDE:
        return np.ones(k)
    levels = np.array([10, -10, 5, -5, 0])
    if k % 512:
        return np.exp2(np.random.permutation(np.resize(levels, k // 32))).repeat(32)
    a = np.empty((k // 512, 16))
    for p in range(k // 512):
        a[p, :8] = np.random.permutation(np.resize(levels, 8))
        for g in range(8):
            far = levels[np.abs(levels - a[p, g]) >= 10]
            a[p, g + 8] = far[np.random.randint(len(far))]
    return np.exp2(a.ravel()).repeat(32)


def f64(x):
    return np.asarray(x).astype(np.float64)


def striped(idx):
    return np.tile(idx.reshape(-1, 16).T, (8, 1)).astype(np.uint16)


def unstriped(offs):
    return offs[:16].T.reshape(-1).astype(np.int64)


def striped8(idx):
    return np.concatenate([x.reshape(-1, 16).T for x in idx]).astype(np.uint16)


def runs(offs, k):
    lists = np.stack([offs[16 * r : 16 * r + 16].T.reshape(-1) for r in range(8)]).astype(np.int64)
    return lists[np.arange(k) % 512 // 64]


def pack_weight(w):
    k, n = w.shape
    w = f64(np.asarray(w, np.float32).astype(ml_dtypes.bfloat16)).reshape(k // 32, 32, n)
    amax = np.abs(w).max(1)
    byte = np.clip(np.where(amax > 0, np.frexp(amax)[1] - 1 + 127 - 7, 1), 1, 254)
    scaled = (w * np.exp2(127.0 - byte)[:, None, :]).reshape(k, n).astype(np.float32)
    words = np.ascontiguousarray(scaled.reshape(k // 512, 128, 4, n).transpose(0, 1, 3, 2)).astype(ml_dtypes.float8_e4m3fn).view(np.uint8)
    return words, np.ascontiguousarray(byte.astype(np.uint8).reshape(k // 512, 16, n))


def unpack_weight(words, scales):
    g, p, n, _ = words.shape
    vals = np.ascontiguousarray(words).view(ml_dtypes.float8_e4m3fn).astype(np.float64) * np.repeat(np.exp2(scales.astype(np.float64) - 127.0), 8, axis=1)[..., None]
    return vals.transpose(0, 1, 3, 2).reshape(g * 512, n)


def sigmoid(v):
    return 1.0 / (1.0 + np.exp(-np.maximum(v, -700.0)))


K, T, S, N, H = 512, 2048, 512, 512, 512


def setup_inputs():
    n = np.random.standard_normal
    s = mx_kscale(K)[:, None]
    u = mx_kscale(S)
    packed_xT = pack_weight(n((K, T)) * s)
    return {
        "x_words": packed_xT[0],
        "x_scales": packed_xT[1],
        "wa": (n((K, H)) / np.sqrt(K) / s).astype(np.float32),
        "wb": (n((K, N)) / np.sqrt(K) / s).astype(np.float32),
        "gt": (np.random.uniform(0.5, 1.5, (S, 1)) * u[:, None]).astype(np.float32),
        "gi": (np.random.uniform(0.5, 1.5, (S, 1)) / u[:, None]).astype(np.float32),
        "offs": striped(np.random.permutation(T)[:S]),
        "two": striped(np.random.permutation(T)[:S]),
        "n1": striped(np.random.permutation(H)),
        "n2": striped(np.random.permutation(H)),
        "n3": striped8(np.stack([np.random.permutation(N) for _ in range(8)])),
        "n4": striped8(np.stack([np.random.permutation(N) for _ in range(8)])),
        "n5": striped8(np.stack([np.random.permutation(N) for _ in range(8)])),
    }


def reference(x_words, x_scales, wa, wb, gt, gi, offs, two, n1, n2, n3, n4, n5):
    xq = unpack_weight(x_words, x_scales)[:, unstriped(offs)]
    a = xq.T @ mxq(f64(wa), 0, "e4m3")
    z = f64(gt) * (a + (sigmoid(a[:, unstriped(n1)])) * (a[:, unstriped(n2)] - a))
    x_two = unpack_weight(x_words, x_scales)[:, unstriped(two)]
    b = x_two.T @ mxq(f64(wb), 0, "e4m3")
    z2 = f64(gi) * b
    cv = 0.0625 * ((mxq(z, 0, "e4m3").T @ mxq(z2, 0, "e4m3")))
    return cv + cv[np.arange(H)[:, None], runs(n3, H)] - (np.maximum(cv[np.arange(H)[:, None], runs(n4, H)], cv[np.arange(H)[:, None], runs(n5, H)]))

@@ -1,0 +1,260 @@
+from contextlib import ExitStack
+
+import concourse.mybir as mybir
+
+K, T, S, H, N = 512, 2048, 512, 512, 512
+FLOPS = 2 * K * S * H + 2 * K * S * N + 2 * S * H * N
+
+F32 = mybir.dt.float32
+BF16 = mybir.dt.bfloat16
+I32 = mybir.dt.int32
+U32 = mybir.dt.uint32
+U16 = mybir.dt.uint16
+U8 = mybir.dt.uint8
+FP8X4 = mybir.dt.float8_e4m3fn_x4
+ALU = mybir.AluOpType
+ACT = mybir.ActivationFunctionType
+
+P = 128
+PACK = 4
+WINDOW = 1024
+CV_SCALE = 0.0625
+
+
+def tile_picked_momtracktrim_none_p_kernel(
+    tc, x_words, x_scales, wa, wb, gt, gi, offs, two, n1, n2, n3, n4, n5, out
+):
+    nc = tc.nc
+    with ExitStack() as ctx:
+        keep = ctx.enter_context(tc.tile_pool(name="keep", bufs=1))
+        psum = ctx.enter_context(tc.psum_pool(name="psum", bufs=1))
+
+        def load_list(name, source):
+            offsets = keep.tile([P, S // 16], U16, name=name)
+            nc.sync.dma_start(offsets[:], source)
+            return offsets
+
+        def interleave(copy, raw, cols, name, tag=""):
+            width = cols.stop - cols.start
+            grouped = keep.tile([P, width * PACK], BF16, name=name, tag=tag, align_bytes=64)
+            copy(
+                grouped[:].rearrange("p (c i j) -> p c j i", i=4, j=PACK),
+                raw[:, :, cols].rearrange("p j (c i) -> p c j i", i=4),
+            )
+            return grouped
+
+        def mx_tiles(name, width, tag=""):
+            codes = keep.tile([P, width], U32, name=name + "_codes", tag=tag, align_bytes=64)
+            scales = keep.tile([P, width], U8, name=name + "_scales", align_bytes=64)
+            return codes, scales
+
+        def quantize(operand, cols, grouped):
+            nc.vector.quantize_mx(out=operand[0][:, cols].bitcast(FP8X4), scales=operand[1][:, cols], in_=grouped)
+
+        def matmul(acc, lhs, lhs_cols, rhs, rhs_cols):
+            nc.tensor.matmul_mx(
+                out=acc,
+                lhsT=lhs[0][:, lhs_cols].bitcast(FP8X4),
+                lhsT_scale=lhs[1][:, lhs_cols],
+                rhs=rhs[0][:, rhs_cols].bitcast(FP8X4),
+                rhs_scale=rhs[1][:, rhs_cols],
+                start=True,
+                stop=True,
+            )
+
+        def dealt(tile):
+            return tile[:].rearrange("p (t m) -> p m t", t=PACK)
+
+        def block(i):
+            return slice(P * i, P * (i + 1))
+
+        def pieces(i):
+            if i == PACK - 1:
+                return [slice(0, H // 2), slice(H // 2, H)]
+            return [slice(0, H)]
+
+        def entries(offsets, cols):
+            return offsets[:, cols.start // 16 : cols.stop // 16]
+
+        table_scales = keep.tile([P, T], U8, name="table_scales", align_bytes=64)
+        nc.vector.memset(table_scales[:].bitcast(I32), 0)
+        offs_sb = load_list("offs_sb", offs)
+        two_sb = load_list("two_sb", two)
+        wa_rows = wa.rearrange("(p j) c -> p j c", j=PACK)
+        wa_raw = [keep.tile([P, PACK, H // 2], F32, name="wa_raw%d" % half) for half in range(2)]
+        nc.sync.dma_start(wa_raw[0][:], wa_rows[:, :, : H // 2])
+        for q in range(4):
+            nc.sync.dma_start(
+                table_scales[32 * q : 32 * q + 4, :].bitcast(I32), x_scales[0, 4 * q : 4 * q + 4, :].bitcast(I32)
+            )
+        nc.sync.dma_start(wa_raw[1][:], wa_rows[:, :, H // 2 :])
+        table_words = keep.tile([P, T], I32, name="table_words", align_bytes=64)
+        nc.sync.dma_start(table_words[:], x_words[0].rearrange("p n t -> p (n t)").bitcast(I32))
+        n2_sb = load_list("n2_sb", n2)
+        n1_sb = load_list("n1_sb", n1)
+        wb_raw = keep.tile([P, PACK, N], F32, name="wb_raw")
+        nc.sync.dma_start(wb_raw[:], wb.rearrange("(p j) c -> p j c", j=PACK))
+        gt_sb = keep.tile([P, PACK], F32, name="gt_sb")
+        nc.sync.dma_start(gt_sb[:], gt.rearrange("(p t) o -> p (t o)", t=PACK))
+        gi_sb = keep.tile([P, PACK], F32, name="gi_sb")
+        nc.sync.dma_start(gi_sb[:], gi.rearrange("(p t) o -> p (t o)", t=PACK))
+        n5_sb = load_list("n5_sb", n5)
+        n3_sb = load_list("n3_sb", n3)
+        n4_sb = load_list("n4_sb", n4)
+
+        windows = []
+        for t in range(PACK):
+            window = keep.tile([P, WINDOW], F32, name="window%d" % t)
+            nc.gpsimd.memset(window[:, H:], 0.0)
+            windows.append(window)
+
+        xa = mx_tiles("xa", S)
+        xb_scales = keep.tile([P, S], U8, name="xb_scales", align_bytes=64)
+        nc.vector.tensor_copy(dealt(xa[1]), table_scales[:].indirect(offs_sb[:]))
+        nc.vector.tensor_copy(dealt(xb_scales), table_scales[:].indirect(two_sb[:]))
+        wa_q = mx_tiles("wa", H)
+        for half in range(2):
+            grouped = interleave(nc.scalar.copy, wa_raw[half], slice(0, H // 2), "wa_g%d" % half)
+            quantize(wa_q, slice(half * H // 2, (half + 1) * H // 2), grouped[:])
+
+        nc.vector.tensor_copy(dealt(xa[0]), table_words[:].bitcast(U32).indirect(offs_sb[:]))
+        a_banks = [psum.tile([P, H], F32, name="a_bank%d" % t) for t in range(PACK)]
+        for t in range(PACK):
+            matmul(a_banks[t][:], xa, block(t), wa_q, slice(0, H))
+
+        xb = (keep.tile([P, S], U32, name="xb_codes", tag="xb_then_move0", align_bytes=64), xb_scales)
+        nc.vector.tensor_copy(dealt(xb[0]), table_words[:].bitcast(U32).indirect(two_sb[:]))
+        wb_q = mx_tiles("wb", N)
+        wb_g = interleave(nc.vector.tensor_copy, wb_raw, slice(0, N), "wb_g")
+
+        z = keep.tile([P, PACK, H], BF16, name="z")
+        gates, picked, diffs, moves = [], [], [], []
+
+        def look_up_a(t):
+            nc.scalar.copy(windows[t][:, :H], a_banks[t][:])
+            other = keep.tile([P, H], F32, name="other%d" % t)
+            gate = keep.tile([P, H], F32, name="gate%d" % t)
+            nc.scalar.activation(other[:], windows[t][:].indirect(n2_sb[:]), ACT.Copy)
+            for cols in pieces(t):
+                nc.scalar.activation(gate[:, cols], windows[t][:].indirect(entries(n1_sb, cols)), ACT.Sigmoid)
+            picked.append(other)
+            gates.append(gate)
+
+        def difference(t):
+            diff = keep.tile([P, H], F32, name="diff%d" % t)
+            nc.gpsimd.tensor_tensor(diff[:], picked[t][:], windows[t][:, :H], ALU.subtract)
+            diffs.append(diff)
+
+        def gated(t):
+            if t == 0:
+                move = keep.tile([P, H], F32, name="move0", tag="xb_then_move0", align_bytes=64)
+            else:
+                move = keep.tile([P, H], F32, name="move%d" % t)
+            for cols in pieces(t):
+                nc.vector.scalar_tensor_tensor(
+                    move[:, cols], diffs[t][:, cols], gt_sb[:, t : t + 1], gates[t][:, cols], ALU.mult, ALU.mult
+                )
+            moves.append(move)
+
+        def finish_z(t):
+            for cols in pieces(t):
+                nc.vector.scalar_tensor_tensor(
+                    z[:, t, cols], a_banks[t][:, cols], gt_sb[:, t : t + 1], moves[t][:, cols], ALU.mult, ALU.add
+                )
+
+        z2_g = keep.tile([P, N * PACK], BF16, name="z2_g", align_bytes=64)
+        b_banks = []
+
+        def project_b(c):
+            bank = psum.tile([P, PACK, P], F32, name="b_bank%d" % c, tag="late_bank%d" % c)
+            for t in range(PACK):
+                matmul(bank[:, t, :], xb, block(t), wb_q, block(c))
+            b_banks.append(bank)
+
+        def weigh_b(c):
+            nc.vector.tensor_tensor(
+                z2_g[:, PACK * P * c : PACK * P * (c + 1)].rearrange("p (n t) -> p n t", t=PACK),
+                b_banks[c][:].rearrange("p t n -> p n t"),
+                gi_sb[:].unsqueeze(1).to_broadcast([P, P, PACK]),
+                ALU.mult,
+            )
+
+        for t in range(PACK):
+            look_up_a(t)
+        for t in range(PACK):
+            difference(t)
+        quantize(wb_q, slice(0, N), wb_g[:])
+        for c in range(PACK):
+            project_b(c)
+        z2_q = mx_tiles("z2", N)
+        for c in range(PACK):
+            weigh_b(c)
+        gated(0)
+        quantize(z2_q, slice(0, N), z2_g[:])
+        finish_z(0)
+        for t in range(1, PACK):
+            gated(t)
+            finish_z(t)
+
+        z_q = mx_tiles("z", H)
+        z_groups = []
+        for u in range(PACK):
+            grouped = keep.tile([P, P * PACK], BF16, name="z_g%d" % u, align_bytes=64)
+            copy = nc.scalar.copy if u in (1, 2) else nc.vector.tensor_copy
+            copy(
+                grouped[:].rearrange("p (c t) -> p c t", t=PACK),
+                z[:].rearrange("p t (c u) -> p u c t", u=PACK)[:, u],
+            )
+            z_groups.append(grouped)
+        cv_banks = []
+        for u in range(PACK):
+            quantize(z_q, block(u), z_groups[u][:])
+            bank = psum.tile([P, N], F32, name="cv_bank%d" % u, tag="late_bank%d" % u)
+            matmul(bank[:], z_q, block(u), z2_q, slice(0, N))
+            cv_banks.append(bank)
+
+        out_rows = out.rearrange("(p u) n -> p u n", u=PACK)
+        at3, at4, at5, sums, larger = [], [], [], [], []
+
+        def scalar_look_ups(u):
+            if u in (0, PACK - 1):
+                nc.scalar.activation(windows[u][:, :N], cv_banks[u][:], ACT.Copy, scale=CV_SCALE)
+            values = keep.tile([P, N], F32, name="at3_%d" % u)
+            nc.scalar.activation(values[:], windows[u][:].indirect(n3_sb[:]), ACT.Copy)
+            at3.append(values)
+            values = keep.tile([P, N], F32, name="at5_%d" % u)
+            for cols in pieces(u):
+                nc.scalar.activation(values[:, cols], windows[u][:].indirect(entries(n5_sb, cols)), ACT.Copy)
+            at5.append(values)
+
+        def vector_look_up(u):
+            values = keep.tile([P, N], F32, name="at4_%d" % u)
+            nc.vector.tensor_copy(values[:], windows[u][:].indirect(n4_sb[:]))
+            at4.append(values)
+
+        def combine(u):
+            total = keep.tile([P, N], F32, name="sum%d" % u)
+            nc.gpsimd.tensor_tensor(total[:], windows[u][:, :N], at3[u][:], ALU.add)
+            sums.append(total)
+            top = keep.tile([P, N], F32, name="larger%d" % u)
+            for cols in pieces(u):
+                nc.vector.tensor_tensor(top[:, cols], at4[u][:, cols], at5[u][:, cols], ALU.max)
+            larger.append(top)
+
+        def store(u):
+            result = keep.tile([P, N], F32, name="result%d" % u)
+            for cols in pieces(u):
+                nc.vector.tensor_tensor(result[:, cols], sums[u][:, cols], larger[u][:, cols], ALU.subtract)
+                nc.sync.dma_start(out_rows[:, u, cols], result[:, cols])
+
+        scalar_look_ups(0)
+        vector_look_up(0)
+        for u in range(1, PACK - 1):
+            nc.vector.tensor_scalar_mul(windows[u][:, :N], cv_banks[u][:], CV_SCALE)
+        for u in range(1, PACK):
+            scalar_look_ups(u)
+        for u in range(PACK):
+            combine(u)
+            if u + 1 < PACK:
+                vector_look_up(u + 1)
+            store(u)

@@ -102,6 +102,9 @@ def tile_picked_momtracktrim_none_p_kernel(
         n3_sb = load_list("n3_sb", n3)
         n4_sb = load_list("n4_sb", n4)
 
+        warm = keep.tile([P, 2], F32, name="warm")
+        nc.gpsimd.memset(warm[:, 0:1], 0.0)
+        nc.scalar.activation(warm[:, 1:2], warm[:, 0:1], ACT.Sigmoid)
         windows = []
         for t in range(PACK):
             window = keep.tile([P, WINDOW], F32, name="window%d" % t)

@@ -43,9 +43,9 @@ def tile_picked_momtracktrim_none_p_kernel(
             )
             return grouped
 
-        def mx_tiles(name, width, tag=""):
-            codes = keep.tile([P, width], U32, name=name + "_codes", tag=tag, align_bytes=64)
-            scales = keep.tile([P, width], U8, name=name + "_scales", align_bytes=64)
+        def mx_tiles(name, width, codes_tag="", scales_tag=""):
+            codes = keep.tile([P, width], U32, name=name + "_codes", tag=codes_tag, align_bytes=64)
+            scales = keep.tile([P, width], U8, name=name + "_scales", tag=scales_tag, align_bytes=64)
             return codes, scales
 
         def quantize(operand, cols, grouped):
@@ -88,12 +88,14 @@ def tile_picked_momtracktrim_none_p_kernel(
                 table_scales[32 * q : 32 * q + 4, :].bitcast(I32), x_scales[0, 4 * q : 4 * q + 4, :].bitcast(I32)
             )
         nc.sync.dma_start(wa_raw[1][:], wa_rows[:, :, H // 2 :])
-        table_words = keep.tile([P, T], I32, name="table_words", align_bytes=64)
+        table_words = keep.tile([P, T], I32, name="table_words", tag="words_xb", align_bytes=64)
         nc.sync.dma_start(table_words[:], x_words[0].rearrange("p n t -> p (n t)").bitcast(I32))
         n2_sb = load_list("n2_sb", n2)
         n1_sb = load_list("n1_sb", n1)
-        wb_raw = keep.tile([P, PACK, N], F32, name="wb_raw")
-        nc.sync.dma_start(wb_raw[:], wb.rearrange("(p j) c -> p j c", j=PACK))
+        wb_rows = wb.rearrange("(p j) c -> p j c", j=PACK)
+        wb_raw = [keep.tile([P, PACK, N // 2], F32, name="wb_raw%d" % half) for half in range(2)]
+        nc.sync.dma_start(wb_raw[0][:], wb_rows[:, :, : N // 2])
+        nc.sync.dma_start(wb_raw[1][:], wb_rows[:, :, N // 2 :])
         gt_sb = keep.tile([P, PACK], F32, name="gt_sb")
         nc.sync.dma_start(gt_sb[:], gt.rearrange("(p t) o -> p (t o)", t=PACK))
         gi_sb = keep.tile([P, PACK], F32, name="gi_sb")
@@ -112,12 +114,11 @@ def tile_picked_momtracktrim_none_p_kernel(
             windows.append(window)
 
         xa = mx_tiles("xa", S)
-        xb_scales = keep.tile([P, S], U8, name="xb_scales", align_bytes=64)
         nc.vector.tensor_copy(dealt(xa[1]), table_scales[:].indirect(offs_sb[:]))
-        nc.vector.tensor_copy(dealt(xb_scales), table_scales[:].indirect(two_sb[:]))
         wa_q = mx_tiles("wa", H)
         for half in range(2):
-            grouped = interleave(nc.scalar.copy, wa_raw[half], slice(0, H // 2), "wa_g%d" % half)
+            tag = "wa_g1_xb_move0" if half else ""
+            grouped = interleave(nc.scalar.copy, wa_raw[half], slice(0, H // 2), "wa_g%d" % half, tag=tag)
             quantize(wa_q, slice(half * H // 2, (half + 1) * H // 2), grouped[:])
 
         nc.vector.tensor_copy(dealt(xa[0]), table_words[:].bitcast(U32).indirect(offs_sb[:]))
@@ -125,39 +126,48 @@ def tile_picked_momtracktrim_none_p_kernel(
         for t in range(PACK):
             matmul(a_banks[t][:], xa, block(t), wa_q, slice(0, H))
 
-        xb = (keep.tile([P, S], U32, name="xb_codes", tag="xb_then_move0", align_bytes=64), xb_scales)
+        xb = mx_tiles("xb", S, codes_tag="wa_g1_xb_move0", scales_tag="words_xb")
         nc.vector.tensor_copy(dealt(xb[0]), table_words[:].bitcast(U32).indirect(two_sb[:]))
-        wb_q = mx_tiles("wb", N)
-        wb_g = interleave(nc.vector.tensor_copy, wb_raw, slice(0, N), "wb_g")
+        wb_q = mx_tiles("wb", N, codes_tag="wb_move1", scales_tag="wb_diff3")
+        wb_g0 = interleave(nc.vector.tensor_copy, wb_raw[0], slice(0, N // 2), "wb_g0")
+        nc.vector.tensor_copy(dealt(xb[1]), table_scales[:].indirect(two_sb[:]))
+        quantize(wb_q, slice(0, N // 2), wb_g0[:])
+        wb_g1 = interleave(nc.vector.tensor_copy, wb_raw[1], slice(0, N // 2), "wb_g1")
 
         z = keep.tile([P, PACK, H], BF16, name="z")
-        gates, picked, diffs, moves = [], [], [], []
+        gates, picked, diffs, moves = {}, {}, {}, {}
 
-        def look_up_a(t):
+        def fill_a(t):
             nc.scalar.copy(windows[t][:, :H], a_banks[t][:])
+
+        def look_up_other(t):
             other = keep.tile([P, H], F32, name="other%d" % t)
-            gate = keep.tile([P, H], F32, name="gate%d" % t)
             nc.scalar.activation(other[:], windows[t][:].indirect(n2_sb[:]), ACT.Copy)
+            picked.setdefault(t, other)
+
+        def look_up_gate(t):
+            gate = keep.tile([P, H], F32, name="gate%d" % t)
             for cols in pieces(t):
                 nc.scalar.activation(gate[:, cols], windows[t][:].indirect(entries(n1_sb, cols)), ACT.Sigmoid)
-            picked.append(other)
-            gates.append(gate)
+            gates.setdefault(t, gate)
 
         def difference(t):
-            diff = keep.tile([P, H], F32, name="diff%d" % t)
-            nc.gpsimd.tensor_tensor(diff[:], picked[t][:], windows[t][:, :H], ALU.subtract)
-            diffs.append(diff)
+            tag = "wb_diff3" if t == PACK - 1 else ""
+            diff = keep.tile([P, H], F32, name="diff%d" % t, tag=tag, align_bytes=64)
+            if t < PACK - 1:
+                nc.gpsimd.tensor_tensor(diff[:], picked[t][:], windows[t][:, :H], ALU.subtract)
+            else:
+                nc.vector.tensor_tensor(diff[:], picked[t][:], a_banks[t][:], ALU.subtract)
+            diffs.setdefault(t, diff)
 
         def gated(t):
-            if t == 0:
-                move = keep.tile([P, H], F32, name="move0", tag="xb_then_move0", align_bytes=64)
-            else:
-                move = keep.tile([P, H], F32, name="move%d" % t)
+            tag = ("wa_g1_xb_move0", "wb_move1", "", "")[t]
+            move = keep.tile([P, H], F32, name="move%d" % t, tag=tag, align_bytes=64)
             for cols in pieces(t):
                 nc.vector.scalar_tensor_tensor(
                     move[:, cols], diffs[t][:, cols], gt_sb[:, t : t + 1], gates[t][:, cols], ALU.mult, ALU.mult
                 )
-            moves.append(move)
+            moves.setdefault(t, move)
 
         def finish_z(t):
             for cols in pieces(t):
@@ -182,82 +192,127 @@ def tile_picked_momtracktrim_none_p_kernel(
                 ALU.mult,
             )
 
-        for t in range(PACK):
-            look_up_a(t)
-        for t in range(PACK):
-            difference(t)
-        quantize(wb_q, slice(0, N), wb_g[:])
-        for c in range(PACK):
-            project_b(c)
+        for step in (fill_a, look_up_other, difference):
+            for t in range(2):
+                step(t)
+        look_up_gate(0)
+        fill_a(2)
+        look_up_other(2)
+        difference(2)
+        look_up_gate(1)
+        look_up_gate(2)
+        fill_a(3)
+        look_up_other(3)
+        look_up_gate(3)
+        project_b(0)
+        project_b(1)
+        weigh_b(0)
+        quantize(wb_q, slice(N // 2, N), wb_g1[:])
+        project_b(2)
+        project_b(3)
         z2_q = mx_tiles("z2", N)
-        for c in range(PACK):
+        for c in range(1, PACK):
             weigh_b(c)
         gated(0)
         quantize(z2_q, slice(0, N), z2_g[:])
         finish_z(0)
-        for t in range(1, PACK):
-            gated(t)
-            finish_z(t)
+        gated(1)
+        finish_z(1)
+        gated(2)
+        difference(3)
+        finish_z(2)
+        gated(3)
+        finish_z(3)
 
         z_q = mx_tiles("z", H)
-        z_groups = []
-        for u in range(PACK):
-            grouped = keep.tile([P, P * PACK], BF16, name="z_g%d" % u, align_bytes=64)
-            copy = nc.scalar.copy if u in (1, 2) else nc.vector.tensor_copy
+        z_groups = [keep.tile([P, P * PACK], BF16, name="z_g%d" % u, align_bytes=64) for u in range(PACK)]
+
+        def group_z(copy, u, half):
+            cols = slice(half * H // 2, (half + 1) * H // 2)
             copy(
-                grouped[:].rearrange("p (c t) -> p c t", t=PACK),
-                z[:].rearrange("p t (c u) -> p u c t", u=PACK)[:, u],
+                z_groups[u][:, cols].rearrange("p (c t) -> p c t", t=PACK),
+                z[:, :, cols].rearrange("p t (c u) -> p u c t", u=PACK)[:, u],
             )
-            z_groups.append(grouped)
+
         cv_banks = []
-        for u in range(PACK):
+
+        def moments(u):
             quantize(z_q, block(u), z_groups[u][:])
             bank = psum.tile([P, N], F32, name="cv_bank%d" % u, tag="late_bank%d" % u)
             matmul(bank[:], z_q, block(u), z2_q, slice(0, N))
             cv_banks.append(bank)
 
+        for u in range(PACK):
+            group_z(nc.scalar.copy, u, 0)
+        for pair in range(2):
+            for u in (2 * pair, 2 * pair + 1):
+                group_z(nc.vector.tensor_copy, u, 1)
+            for u in (2 * pair, 2 * pair + 1):
+                moments(u)
+
         out_rows = out.rearrange("(p u) n -> p u n", u=PACK)
-        at3, at4, at5, sums, larger = [], [], [], [], []
+        at3, at4, at5, larger, rest = {}, {}, {}, {}, {}
 
-        def scalar_look_ups(u):
-            if u in (0, PACK - 1):
+        def fill_cv(u):
+            if u == 1:
+                nc.vector.tensor_scalar_mul(windows[u][:, :N], cv_banks[u][:], CV_SCALE)
+            else:
                 nc.scalar.activation(windows[u][:, :N], cv_banks[u][:], ACT.Copy, scale=CV_SCALE)
-            values = keep.tile([P, N], F32, name="at3_%d" % u)
-            nc.scalar.activation(values[:], windows[u][:].indirect(n3_sb[:]), ACT.Copy)
-            at3.append(values)
-            values = keep.tile([P, N], F32, name="at5_%d" % u)
-            for cols in pieces(u):
-                nc.scalar.activation(values[:, cols], windows[u][:].indirect(entries(n5_sb, cols)), ACT.Copy)
-            at5.append(values)
 
-        def vector_look_up(u):
+        def look_up_n3(u):
+            values = keep.tile([P, N], F32, name="at3_%d" % u)
+            for cols in pieces(u):
+                nc.scalar.activation(values[:, cols], windows[u][:].indirect(entries(n3_sb, cols)), ACT.Copy)
+            at3.setdefault(u, values)
+
+        def look_up_n5(u):
+            values = keep.tile([P, N], F32, name="at5_%d" % u)
+            nc.scalar.activation(values[:], windows[u][:].indirect(n5_sb[:]), ACT.Copy)
+            at5.setdefault(u, values)
+
+        def look_up_n4(u):
             values = keep.tile([P, N], F32, name="at4_%d" % u)
             nc.vector.tensor_copy(values[:], windows[u][:].indirect(n4_sb[:]))
-            at4.append(values)
+            at4.setdefault(u, values)
 
-        def combine(u):
-            total = keep.tile([P, N], F32, name="sum%d" % u)
-            nc.gpsimd.tensor_tensor(total[:], windows[u][:, :N], at3[u][:], ALU.add)
-            sums.append(total)
+        def take_larger(u):
             top = keep.tile([P, N], F32, name="larger%d" % u)
-            for cols in pieces(u):
-                nc.vector.tensor_tensor(top[:, cols], at4[u][:, cols], at5[u][:, cols], ALU.max)
-            larger.append(top)
+            nc.vector.tensor_tensor(top[:], at4[u][:], at5[u][:], ALU.max)
+            larger.setdefault(u, top)
+
+        def subtract_larger(u):
+            left = keep.tile([P, N], F32, name="rest%d" % u)
+            nc.vector.scalar_tensor_tensor(left[:], cv_banks[u][:], CV_SCALE, larger[u][:], ALU.mult, ALU.subtract)
+            rest.setdefault(u, left)
 
         def store(u):
             result = keep.tile([P, N], F32, name="result%d" % u)
+            engine = nc.gpsimd if u < 2 else nc.vector
             for cols in pieces(u):
-                nc.vector.tensor_tensor(result[:, cols], sums[u][:, cols], larger[u][:, cols], ALU.subtract)
+                engine.tensor_tensor(result[:, cols], rest[u][:, cols], at3[u][:, cols], ALU.add)
                 nc.sync.dma_start(out_rows[:, u, cols], result[:, cols])
 
-        scalar_look_ups(0)
-        vector_look_up(0)
-        for u in range(1, PACK - 1):
-            nc.vector.tensor_scalar_mul(windows[u][:, :N], cv_banks[u][:], CV_SCALE)
+        fill_cv(0)
+        fill_cv(1)
+        fill_cv(2)
+        look_up_n5(0)
+        look_up_n5(1)
+        fill_cv(3)
+        look_up_n3(0)
+        look_up_n5(2)
+        look_up_n5(3)
         for u in range(1, PACK):
-            scalar_look_ups(u)
+            look_up_n3(u)
+        look_up_n4(0)
+        look_up_n4(1)
+        take_larger(0)
+        look_up_n4(2)
+        take_larger(1)
+        subtract_larger(0)
+        look_up_n4(3)
+        take_larger(2)
+        take_larger(3)
+        for u in range(1, PACK):
+            subtract_larger(u)
         for u in range(PACK):
-            combine(u)
-            if u + 1 < PACK:
-                vector_look_up(u + 1)
             store(u)

from contextlib import ExitStack

import concourse.mybir as mybir

K, T, S, H, N = 512, 2048, 512, 512, 512
FLOPS = 2 * K * S * H + 2 * K * S * N + 2 * S * H * N

F32 = mybir.dt.float32
BF16 = mybir.dt.bfloat16
I32 = mybir.dt.int32
U32 = mybir.dt.uint32
U16 = mybir.dt.uint16
U8 = mybir.dt.uint8
FP8X4 = mybir.dt.float8_e4m3fn_x4
ALU = mybir.AluOpType
ACT = mybir.ActivationFunctionType

P = 128
PACK = 4
WINDOW = 1024
CV_SCALE = 0.0625


def tile_picked_momtracktrim_none_p_kernel(
    tc, x_words, x_scales, wa, wb, gt, gi, offs, two, n1, n2, n3, n4, n5, out
):
    nc = tc.nc
    with ExitStack() as ctx:
        keep = ctx.enter_context(tc.tile_pool(name="keep", bufs=1))
        psum = ctx.enter_context(tc.psum_pool(name="psum", bufs=1))

        def load_list(name, source):
            offsets = keep.tile([P, S // 16], U16, name=name)
            nc.sync.dma_start(offsets[:], source)
            return offsets

        def interleave(copy, raw, cols, name, tag=""):
            width = cols.stop - cols.start
            grouped = keep.tile([P, width * PACK], BF16, name=name, tag=tag, align_bytes=64)
            copy(
                grouped[:].rearrange("p (c i j) -> p c j i", i=4, j=PACK),
                raw[:, :, cols].rearrange("p j (c i) -> p c j i", i=4),
            )
            return grouped

        def mx_tiles(name, width, codes_tag="", scales_tag=""):
            codes = keep.tile([P, width], U32, name=name + "_codes", tag=codes_tag, align_bytes=64)
            scales = keep.tile([P, width], U8, name=name + "_scales", tag=scales_tag, align_bytes=64)
            return codes, scales

        def quantize(operand, cols, grouped):
            nc.vector.quantize_mx(out=operand[0][:, cols].bitcast(FP8X4), scales=operand[1][:, cols], in_=grouped)

        def matmul(acc, lhs, lhs_cols, rhs, rhs_cols):
            nc.tensor.matmul_mx(
                out=acc,
                lhsT=lhs[0][:, lhs_cols].bitcast(FP8X4),
                lhsT_scale=lhs[1][:, lhs_cols],
                rhs=rhs[0][:, rhs_cols].bitcast(FP8X4),
                rhs_scale=rhs[1][:, rhs_cols],
                start=True,
                stop=True,
            )

        def dealt(tile):
            return tile[:].rearrange("p (t m) -> p m t", t=PACK)

        def block(i):
            return slice(P * i, P * (i + 1))

        def pieces(i):
            if i == PACK - 1:
                return [slice(0, H // 2), slice(H // 2, H)]
            return [slice(0, H)]

        def entries(offsets, cols):
            return offsets[:, cols.start // 16 : cols.stop // 16]

        table_scales = keep.tile([P, T], U8, name="table_scales", align_bytes=64)
        nc.vector.memset(table_scales[:].bitcast(I32), 0)
        offs_sb = load_list("offs_sb", offs)
        two_sb = load_list("two_sb", two)
        wa_rows = wa.rearrange("(p j) c -> p j c", j=PACK)
        wa_raw = [keep.tile([P, PACK, H // 2], F32, name="wa_raw%d" % half) for half in range(2)]
        nc.sync.dma_start(wa_raw[0][:], wa_rows[:, :, : H // 2])
        for q in range(4):
            nc.sync.dma_start(
                table_scales[32 * q : 32 * q + 4, :].bitcast(I32), x_scales[0, 4 * q : 4 * q + 4, :].bitcast(I32)
            )
        nc.sync.dma_start(wa_raw[1][:], wa_rows[:, :, H // 2 :])
        table_words = keep.tile([P, T], I32, name="table_words", tag="words_xb", align_bytes=64)
        nc.sync.dma_start(table_words[:], x_words[0].rearrange("p n t -> p (n t)").bitcast(I32))
        n2_sb = load_list("n2_sb", n2)
        n1_sb = load_list("n1_sb", n1)
        wb_rows = wb.rearrange("(p j) c -> p j c", j=PACK)
        wb_raw = [keep.tile([P, PACK, N // 2], F32, name="wb_raw%d" % half) for half in range(2)]
        nc.sync.dma_start(wb_raw[0][:], wb_rows[:, :, : N // 2])
        nc.sync.dma_start(wb_raw[1][:], wb_rows[:, :, N // 2 :])
        gt_sb = keep.tile([P, PACK], F32, name="gt_sb")
        nc.sync.dma_start(gt_sb[:], gt.rearrange("(p t) o -> p (t o)", t=PACK))
        gi_sb = keep.tile([P, PACK], F32, name="gi_sb")
        nc.sync.dma_start(gi_sb[:], gi.rearrange("(p t) o -> p (t o)", t=PACK))
        n5_sb = load_list("n5_sb", n5)
        n3_sb = load_list("n3_sb", n3)
        n4_sb = load_list("n4_sb", n4)

        warm = keep.tile([P, 2], F32, name="warm")
        nc.gpsimd.memset(warm[:, 0:1], 0.0)
        nc.scalar.activation(warm[:, 1:2], warm[:, 0:1], ACT.Sigmoid)
        windows = []
        for t in range(PACK):
            window = keep.tile([P, WINDOW], F32, name="window%d" % t)
            nc.gpsimd.memset(window[:, H:], 0.0)
            windows.append(window)

        xa = mx_tiles("xa", S)
        nc.vector.tensor_copy(dealt(xa[1]), table_scales[:].indirect(offs_sb[:]))
        wa_q = mx_tiles("wa", H)
        for half in range(2):
            tag = "wa_g1_xb_move0" if half else ""
            grouped = interleave(nc.scalar.copy, wa_raw[half], slice(0, H // 2), "wa_g%d" % half, tag=tag)
            quantize(wa_q, slice(half * H // 2, (half + 1) * H // 2), grouped[:])

        nc.vector.tensor_copy(dealt(xa[0]), table_words[:].bitcast(U32).indirect(offs_sb[:]))
        a_banks = [psum.tile([P, H], F32, name="a_bank%d" % t) for t in range(PACK)]
        for t in range(PACK):
            matmul(a_banks[t][:], xa, block(t), wa_q, slice(0, H))

        xb = mx_tiles("xb", S, codes_tag="wa_g1_xb_move0", scales_tag="words_xb")
        nc.vector.tensor_copy(dealt(xb[0]), table_words[:].bitcast(U32).indirect(two_sb[:]))
        wb_q = mx_tiles("wb", N, codes_tag="wb_move1", scales_tag="wb_diff3")
        wb_g0 = interleave(nc.vector.tensor_copy, wb_raw[0], slice(0, N // 2), "wb_g0")
        nc.vector.tensor_copy(dealt(xb[1]), table_scales[:].indirect(two_sb[:]))
        quantize(wb_q, slice(0, N // 2), wb_g0[:])
        wb_g1 = interleave(nc.vector.tensor_copy, wb_raw[1], slice(0, N // 2), "wb_g1")

        z = keep.tile([P, PACK, H], BF16, name="z")
        gates, picked, diffs, moves = {}, {}, {}, {}

        def fill_a(t):
            nc.scalar.copy(windows[t][:, :H], a_banks[t][:])

        def look_up_other(t):
            other = keep.tile([P, H], F32, name="other%d" % t)
            nc.scalar.activation(other[:], windows[t][:].indirect(n2_sb[:]), ACT.Copy)
            picked.setdefault(t, other)

        def look_up_gate(t):
            gate = keep.tile([P, H], F32, name="gate%d" % t)
            for cols in pieces(t):
                nc.scalar.activation(gate[:, cols], windows[t][:].indirect(entries(n1_sb, cols)), ACT.Sigmoid)
            gates.setdefault(t, gate)

        def difference(t):
            tag = "wb_diff3" if t == PACK - 1 else ""
            diff = keep.tile([P, H], F32, name="diff%d" % t, tag=tag, align_bytes=64)
            if t < PACK - 1:
                nc.gpsimd.tensor_tensor(diff[:], picked[t][:], windows[t][:, :H], ALU.subtract)
            else:
                nc.vector.tensor_tensor(diff[:], picked[t][:], a_banks[t][:], ALU.subtract)
            diffs.setdefault(t, diff)

        def gated(t):
            tag = ("wa_g1_xb_move0", "wb_move1", "", "")[t]
            move = keep.tile([P, H], F32, name="move%d" % t, tag=tag, align_bytes=64)
            for cols in pieces(t):
                nc.vector.scalar_tensor_tensor(
                    move[:, cols], diffs[t][:, cols], gt_sb[:, t : t + 1], gates[t][:, cols], ALU.mult, ALU.mult
                )
            moves.setdefault(t, move)

        def finish_z(t):
            for cols in pieces(t):
                nc.vector.scalar_tensor_tensor(
                    z[:, t, cols], a_banks[t][:, cols], gt_sb[:, t : t + 1], moves[t][:, cols], ALU.mult, ALU.add
                )

        z2_g = keep.tile([P, N * PACK], BF16, name="z2_g", align_bytes=64)
        b_banks = []

        def project_b(c):
            bank = psum.tile([P, PACK, P], F32, name="b_bank%d" % c, tag="late_bank%d" % c)
            for t in range(PACK):
                matmul(bank[:, t, :], xb, block(t), wb_q, block(c))
            b_banks.append(bank)

        def weigh_b(c):
            nc.vector.tensor_tensor(
                z2_g[:, PACK * P * c : PACK * P * (c + 1)].rearrange("p (n t) -> p n t", t=PACK),
                b_banks[c][:].rearrange("p t n -> p n t"),
                gi_sb[:].unsqueeze(1).to_broadcast([P, P, PACK]),
                ALU.mult,
            )

        for step in (fill_a, look_up_other, difference):
            for t in range(2):
                step(t)
        look_up_gate(0)
        fill_a(2)
        look_up_other(2)
        difference(2)
        look_up_gate(1)
        look_up_gate(2)
        fill_a(3)
        look_up_other(3)
        look_up_gate(3)
        project_b(0)
        project_b(1)
        weigh_b(0)
        quantize(wb_q, slice(N // 2, N), wb_g1[:])
        project_b(2)
        project_b(3)
        z2_q = mx_tiles("z2", N)
        for c in range(1, PACK):
            weigh_b(c)
        gated(0)
        quantize(z2_q, slice(0, N), z2_g[:])
        finish_z(0)
        gated(1)
        finish_z(1)
        gated(2)
        difference(3)
        finish_z(2)
        gated(3)
        finish_z(3)

        z_q = mx_tiles("z", H)
        z_groups = [keep.tile([P, P * PACK], BF16, name="z_g%d" % u, align_bytes=64) for u in range(PACK)]

        def group_z(copy, u, half):
            cols = slice(half * H // 2, (half + 1) * H // 2)
            copy(
                z_groups[u][:, cols].rearrange("p (c t) -> p c t", t=PACK),
                z[:, :, cols].rearrange("p t (c u) -> p u c t", u=PACK)[:, u],
            )

        cv_banks = []

        def moments(u):
            quantize(z_q, block(u), z_groups[u][:])
            bank = psum.tile([P, N], F32, name="cv_bank%d" % u, tag="late_bank%d" % u)
            matmul(bank[:], z_q, block(u), z2_q, slice(0, N))
            cv_banks.append(bank)

        for u in range(PACK):
            group_z(nc.scalar.copy, u, 0)
        for pair in range(2):
            for u in (2 * pair, 2 * pair + 1):
                group_z(nc.vector.tensor_copy, u, 1)
            for u in (2 * pair, 2 * pair + 1):
                moments(u)

        out_rows = out.rearrange("(p u) n -> p u n", u=PACK)
        at3, at4, at5, larger, rest = {}, {}, {}, {}, {}

        def fill_cv(u):
            if u == 1:
                nc.vector.tensor_scalar_mul(windows[u][:, :N], cv_banks[u][:], CV_SCALE)
            else:
                nc.scalar.activation(windows[u][:, :N], cv_banks[u][:], ACT.Copy, scale=CV_SCALE)

        def look_up_n3(u):
            values = keep.tile([P, N], F32, name="at3_%d" % u)
            for cols in pieces(u):
                nc.scalar.activation(values[:, cols], windows[u][:].indirect(entries(n3_sb, cols)), ACT.Copy)
            at3.setdefault(u, values)

        def look_up_n5(u):
            values = keep.tile([P, N], F32, name="at5_%d" % u)
            nc.scalar.activation(values[:], windows[u][:].indirect(n5_sb[:]), ACT.Copy)
            at5.setdefault(u, values)

        def look_up_n4(u):
            values = keep.tile([P, N], F32, name="at4_%d" % u)
            nc.vector.tensor_copy(values[:], windows[u][:].indirect(n4_sb[:]))
            at4.setdefault(u, values)

        def take_larger(u):
            top = keep.tile([P, N], F32, name="larger%d" % u)
            nc.vector.tensor_tensor(top[:], at4[u][:], at5[u][:], ALU.max)
            larger.setdefault(u, top)

        def subtract_larger(u):
            left = keep.tile([P, N], F32, name="rest%d" % u)
            nc.vector.scalar_tensor_tensor(left[:], cv_banks[u][:], CV_SCALE, larger[u][:], ALU.mult, ALU.subtract)
            rest.setdefault(u, left)

        def store(u):
            result = keep.tile([P, N], F32, name="result%d" % u)
            engine = nc.gpsimd if u < 2 else nc.vector
            for cols in pieces(u):
                engine.tensor_tensor(result[:, cols], rest[u][:, cols], at3[u][:, cols], ALU.add)
                nc.sync.dma_start(out_rows[:, u, cols], result[:, cols])

        fill_cv(0)
        fill_cv(1)
        fill_cv(2)
        look_up_n5(0)
        look_up_n5(1)
        fill_cv(3)
        look_up_n3(0)
        look_up_n5(2)
        look_up_n5(3)
        for u in range(1, PACK):
            look_up_n3(u)
        look_up_n4(0)
        look_up_n4(1)
        take_larger(0)
        look_up_n4(2)
        take_larger(1)
        subtract_larger(0)
        look_up_n4(3)
        take_larger(2)
        take_larger(3)
        for u in range(1, PACK):
            subtract_larger(u)
        for u in range(PACK):
            store(u)
